import numpy as np
import ml_dtypes


def mxq(x, axis, fmt="e4m3"):
    dtype, down = {"e4m3": (ml_dtypes.float8_e4m3fn, 7), "e5m2": (ml_dtypes.float8_e5m2, 14)}[fmt]
    v = np.moveaxis(np.asarray(x, np.float32).astype(ml_dtypes.bfloat16).astype(np.float64), axis, -1)
    blocks = v.reshape(v.shape[:-1] + (-1, 32))
    amax = np.abs(blocks).max(-1, keepdims=True)
    byte = np.maximum(np.where(amax > 0, np.frexp(amax)[1] - 1 + 127, 0) - down, 1)
    scale = np.exp2(byte - 127.0)
    codes = (blocks / scale).astype(np.float32).astype(dtype).astype(np.float64)
    return np.moveaxis((codes * scale).reshape(v.shape), -1, axis)


WIDE = False


def mx_kscale(k):
    if not WIDE:
        return np.ones(k)
    levels = np.array([10, -10, 5, -5, 0])
    if k % 512:
        return np.exp2(np.random.permutation(np.resize(levels, k // 32))).repeat(32)
    a = np.empty((k // 512, 16))
    for p in range(k // 512):
        a[p, :8] = np.random.permutation(np.resize(levels, 8))
        for g in range(8):
            far = levels[np.abs(levels - a[p, g]) >= 10]
            a[p, g + 8] = far[np.random.randint(len(far))]
    return np.exp2(a.ravel()).repeat(32)


def f64(x):
    return np.asarray(x).astype(np.float64)


def striped(idx):
    return np.tile(idx.reshape(-1, 16).T, (8, 1)).astype(np.uint16)


def unstriped(offs):
    return offs[:16].T.reshape(-1).astype(np.int64)


def striped8(idx):
    return np.concatenate([x.reshape(-1, 16).T for x in idx]).astype(np.uint16)


def runs(offs, k):
    lists = np.stack([offs[16 * r : 16 * r + 16].T.reshape(-1) for r in range(8)]).astype(np.int64)
    return lists[np.arange(k) % 512 // 64]


def pack_weight(w):
    k, n = w.shape
    w = f64(np.asarray(w, np.float32).astype(ml_dtypes.bfloat16)).reshape(k // 32, 32, n)
    amax = np.abs(w).max(1)
    byte = np.clip(np.where(amax > 0, np.frexp(amax)[1] - 1 + 127 - 7, 1), 1, 254)
    scaled = (w * np.exp2(127.0 - byte)[:, None, :]).reshape(k, n).astype(np.float32)
    words = np.ascontiguousarray(scaled.reshape(k // 512, 128, 4, n).transpose(0, 1, 3, 2)).astype(ml_dtypes.float8_e4m3fn).view(np.uint8)
    return words, np.ascontiguousarray(byte.astype(np.uint8).reshape(k // 512, 16, n))


def unpack_weight(words, scales):
    g, p, n, _ = words.shape
    vals = np.ascontiguousarray(words).view(ml_dtypes.float8_e4m3fn).astype(np.float64) * np.repeat(np.exp2(scales.astype(np.float64) - 127.0), 8, axis=1)[..., None]
    return vals.transpose(0, 1, 3, 2).reshape(g * 512, n)


def sigmoid(v):
    return 1.0 / (1.0 + np.exp(-np.maximum(v, -700.0)))

def planes(y):
    n, m = y.shape
    v = y.astype(np.float32).astype(ml_dtypes.bfloat16).astype(np.float64).reshape(n // 32, 32, m)
    top = np.abs(v).max(1)
    byte = np.clip(np.where(top > 0, np.frexp(top)[1] - 1 + 127 - 7, 1), 1, 254)
    codes = (v * np.exp2(127.0 - byte)[:, None, :]).reshape(n, m).astype(np.float32).astype(ml_dtypes.float8_e4m3fn).view(np.uint8)
    words = codes.reshape(n // 512, 128, 4, m).transpose(0, 1, 3, 2)
    return np.ascontiguousarray(words), np.ascontiguousarray(byte.astype(np.uint8).reshape(n // 512, 16, m))


K, T, S, H, C = 512, 2048, 512, 512, 512


def setup_inputs():
    n = np.random.standard_normal
    s = mx_kscale(K)[:, None]
    packed_xT = pack_weight(n((K, T)) * s)
    packed_w1 = pack_weight(n((K, H)) / np.sqrt(K) / s)
    return {
        "x_words": packed_xT[0],
        "x_scales": packed_xT[1],
        "w1_words": packed_w1[0],
        "w1_scales": packed_w1[1],
        "gs": (np.random.uniform(0.5, 1.5, (K, 1)) / s).astype(np.float32),
        "offs": striped(np.random.permutation(T)[:S]),
        "n1": striped8(np.stack([np.random.permutation(S) for _ in range(8)])),
        "ca": striped(np.random.permutation(T)[:C]),
        "cb": striped(np.random.permutation(T)[:C]),
        "n2": striped8(np.stack([np.random.permutation(S) for _ in range(8)])),
        "n3": striped8(np.stack([np.random.permutation(S) for _ in range(8)])),
    }


def reference(x_words, x_scales, w1_words, w1_scales, gs, offs, n1, ca, cb, n2, n3):
    x_ca = unpack_weight(x_words, x_scales)[:, unstriped(ca)]
    xq = unpack_weight(x_words, x_scales)[:, unstriped(offs)]
    y = unpack_weight(w1_words, w1_scales).T @ xq
    z = f64(gs) * (y * (sigmoid(y[np.arange(H)[:, None], runs(n1, H)])))
    zq = mxq(z, 0, "e4m3")
    a = 0.0625 * (x_ca.T @ zq)
    x_cb = unpack_weight(x_words, x_scales)[:, unstriped(cb)]
    b = 0.0625 * (x_cb.T @ zq)
    out_0 = a * (sigmoid(b[np.arange(C)[:, None], runs(n3, C)])) - (0.5 * (a[np.arange(C)[:, None], runs(n2, C)]))
    return (out_0,) + planes(out_0)

@@ -1,0 +1,173 @@
+from contextlib import ExitStack
+
+import concourse.mybir as mybir
+
+K, T, S, H, C = 512, 2048, 512, 512, 512
+FLOPS = 2 * K * H * S + 2 * 2 * K * C * S
+
+F32 = mybir.dt.float32
+BF16 = mybir.dt.bfloat16
+I32 = mybir.dt.int32
+U32 = mybir.dt.uint32
+U16 = mybir.dt.uint16
+U8 = mybir.dt.uint8
+FP8X4 = mybir.dt.float8_e4m3fn_x4
+MULT = mybir.AluOpType.mult
+ADD = mybir.AluOpType.add
+SIGMOID = mybir.ActivationFunctionType.Sigmoid
+COPY = mybir.ActivationFunctionType.Copy
+
+P = 128
+PACK = 4
+HALVES = 2
+W = S // HALVES
+LIST_COLS = W // 16
+
+
+def interleave(engine_copy, dst, src):
+    engine_copy(
+        dst.rearrange("p (c i t) -> p c t i", i=4, t=PACK),
+        src.rearrange("p t (c i) -> p c t i", i=4),
+    )
+
+
+def tile_picked_ccmpgatebgate_none_po_kernel(
+    tc, x_words, x_scales, w1_words, w1_scales, gs, offs, n1, ca, cb, n2, n3, out_0, out_1, out_2
+):
+    nc = tc.nc
+    with ExitStack() as ctx:
+        lists = ctx.enter_context(tc.tile_pool(name="lists", bufs=1))
+        keep = ctx.enter_context(tc.tile_pool(name="keep", bufs=1))
+        reuse = ctx.enter_context(tc.tile_pool(name="reuse", bufs=1))
+        psum = ctx.enter_context(tc.psum_pool(name="psum", bufs=1))
+
+        def list_tile(name):
+            return lists.tile([P, S // 16], U16, name=name)
+
+        def sb(name, shape, dtype, tag=None):
+            return keep.tile(shape, dtype, name=name, tag=tag or name, align_bytes=64)
+
+        offs_sb, n1_sb, ca_sb, cb_sb, n2_sb, n3_sb = [list_tile(n) for n in ("offs_sb", "n1_sb", "ca_sb", "cb_sb", "n2_sb", "n3_sb")]
+        xw = sb("xw", [P, T], U32)
+        xs = sb("xs", [P, T], U8)
+        w1w = sb("w1w", [P, H], U32)
+        w1s = reuse.tile([P, H], U8, name="w1s", align_bytes=64, offset=4096)
+        gs_sb = sb("gs_sb", [P, PACK], F32)
+        warm = sb("warm", [P, 2], F32)
+
+        nc.vector.memset(xs[:].bitcast(I32), 0)
+        nc.gpsimd.memset(w1s[:].bitcast(I32), 0)
+        nc.gpsimd.memset(warm[:, 0:1], 0.0)
+        nc.scalar.activation(warm[:, 1:2], warm[:, 0:1], SIGMOID)
+
+        nc.sync.dma_start(offs_sb[:], offs)
+        nc.sync.dma_start(w1w[:].bitcast(I32), w1_words[0].rearrange("p n t -> p (n t)").bitcast(I32))
+        for q in range(4):
+            nc.sync.dma_start(xs[32 * q : 32 * q + 4, :].bitcast(I32), x_scales[0, 4 * q : 4 * q + 4, :].bitcast(I32))
+        nc.sync.dma_start(cb_sb[:], cb)
+        nc.sync.dma_start(xw[:].bitcast(I32), x_words[0].rearrange("p n t -> p (n t)").bitcast(I32))
+        nc.sync.dma_start(ca_sb[:], ca)
+        for q in range(4):
+            nc.sync.dma_start(w1s[32 * q : 32 * q + 4, :].bitcast(I32), w1_scales[0, 4 * q : 4 * q + 4, :].bitcast(I32))
+        nc.sync.dma_start(n1_sb[:], n1)
+        nc.sync.dma_start(n3_sb[:], n3)
+        nc.sync.dma_start(n2_sb[:], n2)
+        nc.gpsimd.dma_start(gs_sb[:], gs.rearrange("(p t) o -> p (t o)", t=PACK))
+
+        def dealt(ap):
+            return ap.rearrange("p (t m) -> p m t", t=PACK)
+
+        def listed(ap):
+            return ap.rearrange("p (m t) -> p m t", t=PACK)
+
+        xq_w = sb("xq_w", [P, S], U32)
+        xq_s = sb("xq_s", [P, S], U8)
+        w1d_w = sb("w1d_w", [P, H], U32)
+        w1d_s = sb("w1d_s", [P, H], U8)
+        cb_g = sb("cb_g", [P, C], U8)
+        cb_s = sb("cb_s", [P, C], U8)
+        ca_s = sb("ca_s", [P, C], U8)
+
+        nc.vector.tensor_copy(xq_s[:], xs[:].indirect(offs_sb[:]))
+        nc.vector.tensor_copy(dealt(w1d_w[:].bitcast(I32)), listed(w1w[:].bitcast(I32)))
+        nc.vector.tensor_copy(xq_w[:], xw[:].indirect(offs_sb[:]))
+        nc.vector.tensor_copy(dealt(w1d_s[:]), listed(w1s[:]))
+        nc.vector.tensor_copy(cb_g[:], xs[:].indirect(cb_sb[:]))
+        nc.vector.tensor_copy(dealt(cb_s[:]), listed(cb_g[:]))
+        pair_w = reuse.tile([P, 2, C], U32, name="pair_w", align_bytes=64, offset=64)
+        ca_g = reuse.tile([P, C], U8, name="ca_g", align_bytes=64, offset=4544)
+        cb_w = pair_w[:, 0, :]
+        ca_w = pair_w[:, 1, :]
+        nc.vector.tensor_copy(dealt(cb_w), xw[:].indirect(cb_sb[:]))
+        nc.vector.tensor_copy(ca_g[:], xs[:].indirect(ca_sb[:]))
+        nc.vector.tensor_copy(dealt(ca_w), xw[:].indirect(ca_sb[:]))
+        nc.vector.tensor_copy(dealt(ca_s[:]), listed(ca_g[:]))
+
+        def product(out, lhs_w, lhs_s, t, rhs_w, rhs_s):
+            cols = slice(t * P, (t + 1) * P)
+            nc.tensor.matmul_mx(
+                out=out,
+                lhsT=lhs_w[:, cols].bitcast(FP8X4),
+                lhsT_scale=lhs_s[:, cols],
+                rhs=rhs_w.bitcast(FP8X4),
+                rhs_scale=rhs_s,
+                start=True,
+                stop=True,
+            )
+
+        y = [sb("y%d" % t, [P, S], F32) for t in range(PACK)]
+        for t in range(PACK):
+            y_ps = psum.tile([P, S], F32, name="y_ps", tag="bank%d" % t)
+            product(y_ps[:], w1d_w, w1d_s, t, xq_w[:], xq_s[:])
+            nc.scalar.copy(y[t][:], y_ps[:])
+
+        b = [sb("b%d" % t, [P, S], F32) for t in range(PACK)]
+        na = [sb("na%d" % t, [P, S], F32) for t in range(PACK)]
+        for h in range(HALVES):
+            cols = slice(h * W, (h + 1) * W)
+            entries = slice(h * LIST_COLS, (h + 1) * LIST_COLS)
+            z = sb("z%d" % h, [P, PACK, W], BF16, tag="z")
+            for t in range(PACK):
+                gate = sb("ygate%d_%d" % (t, h), [P, W], F32)
+                nc.scalar.activation(gate[:], y[t][:].indirect(n1_sb[:, entries]), SIGMOID)
+                nc.vector.scalar_tensor_tensor(z[:, t, :], y[t][:, cols], gs_sb[:, t : t + 1], gate[:], MULT, MULT)
+            zi = sb("zi%d" % h, [P, PACK * W], BF16)
+            interleave(nc.vector.tensor_copy, zi[:], z[:])
+            zq_w = sb("zq_w%d" % h, [P, W], U32)
+            zq_s = sb("zq_s%d" % h, [P, W], U8)
+            nc.vector.quantize_mx(out=zq_w[:].bitcast(FP8X4), scales=zq_s[:], in_=zi[:])
+            banks = [psum.tile([P, 2, W], F32, name="ab_ps", tag="bank%d" % ((4 * (h + 1) + i) % 8)) for i in range(4)]
+            for t in range(PACK):
+                product(banks[t // 2][:, t % 2, :], cb_w, cb_s, t, zq_w[:], zq_s[:])
+            for t in range(PACK):
+                product(banks[2 + t // 2][:, t % 2, :], ca_w, ca_s, t, zq_w[:], zq_s[:])
+            for t in range(PACK):
+                nc.scalar.copy(b[t][:, cols], banks[t // 2][:, t % 2, :])
+            for t in range(PACK):
+                if h == 0:
+                    nc.scalar.activation(na[t][:, cols], banks[2 + t // 2][:, t % 2, :], COPY, scale=-1.0 / 32)
+                else:
+                    nc.vector.tensor_scalar(na[t][:, cols], banks[2 + t // 2][:, t % 2, :], -1.0 / 32, None, MULT)
+
+        o_s = sb("o_s", [P, S], U8)
+        out_rows = out_0.rearrange("(p t) j -> p t j", t=PACK)
+        out_words = out_1[0].rearrange("p n t -> p (n t)").bitcast(I32)
+        for h in range(HALVES):
+            cols = slice(h * W, (h + 1) * W)
+            entries = slice(h * LIST_COLS, (h + 1) * LIST_COLS)
+            o = sb("o%d" % h, [P, PACK, W], F32)
+            for t in range(PACK):
+                gate = sb("bgate%d_%d" % (t, h), [P, W], F32)
+                nc.scalar.activation(gate[:], b[t][:].indirect(n3_sb[:, entries]), SIGMOID, scale=1.0 / 16)
+                gated = sb("gated%d_%d" % (t, h), [P, W], F32)
+                nc.vector.scalar_tensor_tensor(gated[:], na[t][:, cols], -2.0, gate[:], MULT, MULT)
+                nc.vector.tensor_tensor(o[:, t, :], na[t][:].indirect(n2_sb[:, entries]), gated[:], ADD)
+            nc.sync.dma_start(out_rows[:, :, cols], o[:])
+            oi = sb("oi%d" % h, [P, PACK * W], BF16)
+            interleave(nc.scalar.copy if h == 0 else nc.vector.tensor_copy, oi[:], o[:])
+            o_w = sb("o_w%d" % h, [P, W], U32)
+            nc.vector.quantize_mx(out=o_w[:].bitcast(FP8X4), scales=o_s[:, cols], in_=oi[:])
+            nc.sync.dma_start(out_words[:, cols], o_w[:].bitcast(I32))
+        for q in range(4):
+            queue = nc.scalar if q % 2 else nc.sync
+            queue.dma_start(out_2[0, 4 * q : 4 * q + 4, :].bitcast(I32), o_s[32 * q : 32 * q + 4, :].bitcast(I32))

@@ -19,9 +19,21 @@ COPY = mybir.ActivationFunctionType.Copy
 
 P = 128
 PACK = 4
-HALVES = 2
-W = S // HALVES
-LIST_COLS = W // 16
+Y_CHUNKS = (256, 256)
+Y_BANKS = ((4, 5, 6, 7), (0, 1, 2, 7))
+Z_CHUNKS = (256, 256)
+OUT_CHUNKS = (256, 256)
+B_BANKS = ((4, 4, 5, 5), (6, 7, 4, 5))
+PAIRS = ((0, 1), (2, 3))
+
+
+def spans(widths):
+    starts = [sum(widths[:i]) for i in range(len(widths))]
+    return [slice(s, s + w) for s, w in zip(starts, widths)]
+
+
+def entries(cols):
+    return slice(cols.start // 16, cols.stop // 16)
 
 
 def interleave(engine_copy, dst, src):
@@ -38,7 +50,6 @@ def tile_picked_ccmpgatebgate_none_po_kernel(
     with ExitStack() as ctx:
         lists = ctx.enter_context(tc.tile_pool(name="lists", bufs=1))
         keep = ctx.enter_context(tc.tile_pool(name="keep", bufs=1))
-        reuse = ctx.enter_context(tc.tile_pool(name="reuse", bufs=1))
         psum = ctx.enter_context(tc.psum_pool(name="psum", bufs=1))
 
         def list_tile(name):
@@ -51,7 +62,7 @@ def tile_picked_ccmpgatebgate_none_po_kernel(
         xw = sb("xw", [P, T], U32)
         xs = sb("xs", [P, T], U8)
         w1w = sb("w1w", [P, H], U32)
-        w1s = reuse.tile([P, H], U8, name="w1s", align_bytes=64, offset=4096)
+        w1s = sb("w1s", [P, H], U8)
         gs_sb = sb("gs_sb", [P, PACK], F32)
         warm = sb("warm", [P, 2], F32)
 
@@ -70,9 +81,9 @@ def tile_picked_ccmpgatebgate_none_po_kernel(
         for q in range(4):
             nc.sync.dma_start(w1s[32 * q : 32 * q + 4, :].bitcast(I32), w1_scales[0, 4 * q : 4 * q + 4, :].bitcast(I32))
         nc.sync.dma_start(n1_sb[:], n1)
+        nc.sync.dma_start(gs_sb[:], gs.rearrange("(p t) o -> p (t o)", t=PACK))
         nc.sync.dma_start(n3_sb[:], n3)
         nc.sync.dma_start(n2_sb[:], n2)
-        nc.gpsimd.dma_start(gs_sb[:], gs.rearrange("(p t) o -> p (t o)", t=PACK))
 
         def dealt(ap):
             return ap.rearrange("p (t m) -> p m t", t=PACK)
@@ -88,20 +99,20 @@ def tile_picked_ccmpgatebgate_none_po_kernel(
         cb_s = sb("cb_s", [P, C], U8)
         ca_s = sb("ca_s", [P, C], U8)
 
+        def deal(engine, dst, src):
+            engine.tensor_copy(dst.rearrange("p (t m) -> p t m", t=PACK), src.rearrange("p (m t) -> p t m", t=PACK))
+
         nc.vector.tensor_copy(xq_s[:], xs[:].indirect(offs_sb[:]))
-        nc.vector.tensor_copy(dealt(w1d_w[:].bitcast(I32)), listed(w1w[:].bitcast(I32)))
-        nc.vector.tensor_copy(xq_w[:], xw[:].indirect(offs_sb[:]))
-        nc.vector.tensor_copy(dealt(w1d_s[:]), listed(w1s[:]))
+        deal(nc.gpsimd, w1d_w[:].bitcast(I32), w1w[:].bitcast(I32))
+        for cols in spans(Y_CHUNKS):
+            nc.vector.tensor_copy(xq_w[:, cols], xw[:].indirect(offs_sb[:, entries(cols)]))
+        deal(nc.gpsimd, w1d_s[:], w1s[:])
         nc.vector.tensor_copy(cb_g[:], xs[:].indirect(cb_sb[:]))
-        nc.vector.tensor_copy(dealt(cb_s[:]), listed(cb_g[:]))
-        pair_w = reuse.tile([P, 2, C], U32, name="pair_w", align_bytes=64, offset=64)
-        ca_g = reuse.tile([P, C], U8, name="ca_g", align_bytes=64, offset=4544)
-        cb_w = pair_w[:, 0, :]
-        ca_w = pair_w[:, 1, :]
-        nc.vector.tensor_copy(dealt(cb_w), xw[:].indirect(cb_sb[:]))
+        deal(nc.vector, cb_s[:], cb_g[:])
+        cb_w = sb("cb_w", [P, C], U32)
+        ca_g = sb("ca_g", [P, C], U8)
+        nc.vector.tensor_copy(dealt(cb_w[:]), xw[:].indirect(cb_sb[:]))
         nc.vector.tensor_copy(ca_g[:], xs[:].indirect(ca_sb[:]))
-        nc.vector.tensor_copy(dealt(ca_w), xw[:].indirect(ca_sb[:]))
-        nc.vector.tensor_copy(dealt(ca_s[:]), listed(ca_g[:]))
 
         def product(out, lhs_w, lhs_s, t, rhs_w, rhs_s):
             cols = slice(t * P, (t + 1) * P)
@@ -116,56 +127,84 @@ def tile_picked_ccmpgatebgate_none_po_kernel(
             )
 
         y = [sb("y%d" % t, [P, S], F32) for t in range(PACK)]
-        for t in range(PACK):
-            y_ps = psum.tile([P, S], F32, name="y_ps", tag="bank%d" % t)
-            product(y_ps[:], w1d_w, w1d_s, t, xq_w[:], xq_s[:])
-            nc.scalar.copy(y[t][:], y_ps[:])
+        y_bank = {}
+        for h, cols in enumerate(spans(Y_CHUNKS)):
+            for t in range(PACK):
+                i = Y_BANKS[h][t]
+                if i not in y_bank:
+                    y_bank[i] = psum.tile([P, S], F32, name="y_ps", tag="bank%d" % i)
+                product(y_bank[i][:, cols], w1d_w, w1d_s, t, xq_w[:, cols], xq_s[:, cols])
+                if t < PACK - 1:
+                    nc.scalar.copy(y[t][:, cols], y_bank[i][:, cols])
+        nc.vector.tensor_copy(y[PACK - 1][:], y_bank[Y_BANKS[0][PACK - 1]][:])
+
+        ca_w = sb("ca_w", [P, C], U32, tag="xq_w")
+        nc.vector.tensor_copy(dealt(ca_w[:]), xw[:].indirect(ca_sb[:]))
+        deal(nc.vector, ca_s[:], ca_g[:])
+
+        y_gate = {}
+        for h, cols in enumerate(spans(Z_CHUNKS)):
+            for t in range(PACK):
+                y_gate[h, t] = sb("y_gate%d_%d" % (h, t), [P, Z_CHUNKS[h]], F32)
+                nc.scalar.activation(y_gate[h, t][:], y[t][:].indirect(n1_sb[:, entries(cols)]), SIGMOID)
 
         b = [sb("b%d" % t, [P, S], F32) for t in range(PACK)]
         na = [sb("na%d" % t, [P, S], F32) for t in range(PACK)]
-        for h in range(HALVES):
-            cols = slice(h * W, (h + 1) * W)
-            entries = slice(h * LIST_COLS, (h + 1) * LIST_COLS)
-            z = sb("z%d" % h, [P, PACK, W], BF16, tag="z")
+        a_ps = [psum.tile([P, S], F32, name="a_ps", tag="bank%d" % t) for t in range(PACK)]
+        last = len(Z_CHUNKS) - 1
+
+        for h, cols in enumerate(spans(Z_CHUNKS)):
+            w = Z_CHUNKS[h]
+            z = sb("z%d" % h, [P, PACK, w], BF16, tag="z")
             for t in range(PACK):
-                gate = sb("ygate%d_%d" % (t, h), [P, W], F32)
-                nc.scalar.activation(gate[:], y[t][:].indirect(n1_sb[:, entries]), SIGMOID)
-                nc.vector.scalar_tensor_tensor(z[:, t, :], y[t][:, cols], gs_sb[:, t : t + 1], gate[:], MULT, MULT)
-            zi = sb("zi%d" % h, [P, PACK * W], BF16)
+                nc.vector.scalar_tensor_tensor(z[:, t, :], y[t][:, cols], gs_sb[:, t : t + 1], y_gate[h, t][:], MULT, MULT)
+            zi = sb("zi%d" % h, [P, PACK * w], BF16)
             interleave(nc.vector.tensor_copy, zi[:], z[:])
-            zq_w = sb("zq_w%d" % h, [P, W], U32)
-            zq_s = sb("zq_s%d" % h, [P, W], U8)
+            zq_w = sb("zq_w%d" % h, [P, w], U32)
+            zq_s = sb("zq_s%d" % h, [P, w], U8)
             nc.vector.quantize_mx(out=zq_w[:].bitcast(FP8X4), scales=zq_s[:], in_=zi[:])
-            banks = [psum.tile([P, 2, W], F32, name="ab_ps", tag="bank%d" % ((4 * (h + 1) + i) % 8)) for i in range(4)]
-            for t in range(PACK):
-                product(banks[t // 2][:, t % 2, :], cb_w, cb_s, t, zq_w[:], zq_s[:])
-            for t in range(PACK):
-                product(banks[2 + t // 2][:, t % 2, :], ca_w, ca_s, t, zq_w[:], zq_s[:])
-            for t in range(PACK):
-                nc.scalar.copy(b[t][:, cols], banks[t // 2][:, t % 2, :])
-            for t in range(PACK):
-                if h == 0:
-                    nc.scalar.activation(na[t][:, cols], banks[2 + t // 2][:, t % 2, :], COPY, scale=-1.0 / 32)
-                else:
-                    nc.vector.tensor_scalar(na[t][:, cols], banks[2 + t // 2][:, t % 2, :], -1.0 / 32, None, MULT)
+            bank = {}
+            for i in sorted(set(B_BANKS[h])):
+                bank[i] = psum.tile([P, S], F32, name="b_ps", tag="bank%d" % i)
+            b_ps = [bank[B_BANKS[h][t]][:, (t * w) % S : (t * w) % S + w] for t in range(PACK)]
+            for pair in PAIRS:
+                for t in pair:
+                    product(b_ps[t], cb_w, cb_s, t, zq_w[:], zq_s[:])
+                for t in pair:
+                    product(a_ps[t][:, cols], ca_w, ca_s, t, zq_w[:], zq_s[:])
+            if h < last:
+                for t in range(PACK):
+                    nc.scalar.copy(b[t][:, cols], b_ps[t])
+                for t in range(PACK):
+                    nc.scalar.activation(na[t][:, cols], a_ps[t][:, cols], COPY, scale=-1.0 / 32)
+        last_cols, last_b = cols, b_ps
 
         o_s = sb("o_s", [P, S], U8)
         out_rows = out_0.rearrange("(p t) j -> p t j", t=PACK)
         out_words = out_1[0].rearrange("p n t -> p (n t)").bitcast(I32)
-        for h in range(HALVES):
-            cols = slice(h * W, (h + 1) * W)
-            entries = slice(h * LIST_COLS, (h + 1) * LIST_COLS)
-            o = sb("o%d" % h, [P, PACK, W], F32)
-            for t in range(PACK):
-                gate = sb("bgate%d_%d" % (t, h), [P, W], F32)
-                nc.scalar.activation(gate[:], b[t][:].indirect(n3_sb[:, entries]), SIGMOID, scale=1.0 / 16)
-                gated = sb("gated%d_%d" % (t, h), [P, W], F32)
-                nc.vector.scalar_tensor_tensor(gated[:], na[t][:, cols], -2.0, gate[:], MULT, MULT)
-                nc.vector.tensor_tensor(o[:, t, :], na[t][:].indirect(n2_sb[:, entries]), gated[:], ADD)
-            nc.sync.dma_start(out_rows[:, :, cols], o[:])
-            oi = sb("oi%d" % h, [P, PACK * W], BF16)
-            interleave(nc.scalar.copy if h == 0 else nc.vector.tensor_copy, oi[:], o[:])
-            o_w = sb("o_w%d" % h, [P, W], U32)
+        o = [sb("o%d" % h, [P, PACK, w], F32) for h, w in enumerate(OUT_CHUNKS)]
+        for pair in PAIRS:
+            for h, cols in enumerate(spans(OUT_CHUNKS)):
+                w = OUT_CHUNKS[h]
+                for t in pair:
+                    if h == 0:
+                        nc.scalar.copy(b[t][:, last_cols], last_b[t])
+                        if pair == PAIRS[0]:
+                            nc.vector.tensor_scalar(na[t][:, last_cols], a_ps[t][:, last_cols], -1.0 / 32, None, MULT)
+                        else:
+                            nc.scalar.activation(na[t][:, last_cols], a_ps[t][:, last_cols], COPY, scale=-1.0 / 32)
+                    gate = sb("b_gate%d_%d" % (t, h), [P, w], F32)
+                    nc.scalar.activation(gate[:], b[t][:].indirect(n3_sb[:, entries(cols)]), SIGMOID, scale=1.0 / 16)
+                    gated = sb("gated%d_%d" % (t, h), [P, w], F32)
+                    nc.vector.scalar_tensor_tensor(gated[:], na[t][:, cols], -2.0, gate[:], MULT, MULT)
+                    nc.vector.tensor_tensor(o[h][:, t, :], na[t][:].indirect(n2_sb[:, entries(cols)]), gated[:], ADD)
+                rows = slice(pair[0], pair[1] + 1)
+                nc.sync.dma_start(out_rows[:, rows, cols], o[h][:, rows, :])
+        for h, cols in enumerate(spans(OUT_CHUNKS)):
+            w = OUT_CHUNKS[h]
+            oi = sb("oi%d" % h, [P, PACK * w], BF16)
+            interleave(nc.scalar.copy if h < len(OUT_CHUNKS) - 1 else nc.vector.tensor_copy, oi[:], o[h][:])
+            o_w = sb("o_w%d" % h, [P, w], U32)
             nc.vector.quantize_mx(out=o_w[:].bitcast(FP8X4), scales=o_s[:, cols], in_=oi[:])
             nc.sync.dma_start(out_words[:, cols], o_w[:].bitcast(I32))
         for q in range(4):

@@ -20,11 +20,11 @@ COPY = mybir.ActivationFunctionType.Copy
 P = 128
 PACK = 4
 Y_CHUNKS = (256, 256)
-Y_BANKS = ((4, 5, 6, 7), (0, 1, 2, 7))
+Y_BANKS = ((4, 5, 6, 7), (0, 1, 2, 3))
 Z_CHUNKS = (256, 256)
-OUT_CHUNKS = (256, 256)
+GATE_CHUNKS = (256, 256)
+OUT_CHUNKS = (256, 128, 128)
 B_BANKS = ((4, 4, 5, 5), (6, 7, 4, 5))
-PAIRS = ((0, 1), (2, 3))
 
 
 def spans(widths):
@@ -50,6 +50,7 @@ def tile_picked_ccmpgatebgate_none_po_kernel(
     with ExitStack() as ctx:
         lists = ctx.enter_context(tc.tile_pool(name="lists", bufs=1))
         keep = ctx.enter_context(tc.tile_pool(name="keep", bufs=1))
+        reuse = ctx.enter_context(tc.tile_pool(name="reuse", bufs=1))
         psum = ctx.enter_context(tc.psum_pool(name="psum", bufs=1))
 
         def list_tile(name):
@@ -62,7 +63,7 @@ def tile_picked_ccmpgatebgate_none_po_kernel(
         xw = sb("xw", [P, T], U32)
         xs = sb("xs", [P, T], U8)
         w1w = sb("w1w", [P, H], U32)
-        w1s = sb("w1s", [P, H], U8)
+        w1s = reuse.tile([P, H], U8, name="w1s", align_bytes=64, offset=4096)
         gs_sb = sb("gs_sb", [P, PACK], F32)
         warm = sb("warm", [P, 2], F32)
 
@@ -91,7 +92,6 @@ def tile_picked_ccmpgatebgate_none_po_kernel(
         def listed(ap):
             return ap.rearrange("p (m t) -> p m t", t=PACK)
 
-        xq_w = sb("xq_w", [P, S], U32)
         xq_s = sb("xq_s", [P, S], U8)
         w1d_w = sb("w1d_w", [P, H], U32)
         w1d_s = sb("w1d_s", [P, H], U8)
@@ -99,20 +99,22 @@ def tile_picked_ccmpgatebgate_none_po_kernel(
         cb_s = sb("cb_s", [P, C], U8)
         ca_s = sb("ca_s", [P, C], U8)
 
-        def deal(engine, dst, src):
-            engine.tensor_copy(dst.rearrange("p (t m) -> p t m", t=PACK), src.rearrange("p (m t) -> p t m", t=PACK))
-
         nc.vector.tensor_copy(xq_s[:], xs[:].indirect(offs_sb[:]))
-        deal(nc.gpsimd, w1d_w[:].bitcast(I32), w1w[:].bitcast(I32))
-        for cols in spans(Y_CHUNKS):
-            nc.vector.tensor_copy(xq_w[:, cols], xw[:].indirect(offs_sb[:, entries(cols)]))
-        deal(nc.gpsimd, w1d_s[:], w1s[:])
+        nc.vector.tensor_copy(dealt(w1d_w[:].bitcast(I32)), listed(w1w[:].bitcast(I32)))
+        nc.vector.tensor_copy(dealt(w1d_s[:]), listed(w1s[:]))
+        xq_w = [
+            sb("xq_w0", [P, Y_CHUNKS[0]], U32),
+            reuse.tile([P, Y_CHUNKS[1]], U32, name="xq_w1", align_bytes=64, offset=4544),
+        ]
+        for h, cols in enumerate(spans(Y_CHUNKS)):
+            nc.vector.tensor_copy(xq_w[h][:], xw[:].indirect(offs_sb[:, entries(cols)]))
         nc.vector.tensor_copy(cb_g[:], xs[:].indirect(cb_sb[:]))
-        deal(nc.vector, cb_s[:], cb_g[:])
-        cb_w = sb("cb_w", [P, C], U32)
-        ca_g = sb("ca_g", [P, C], U8)
-        nc.vector.tensor_copy(dealt(cb_w[:]), xw[:].indirect(cb_sb[:]))
-        nc.vector.tensor_copy(ca_g[:], xs[:].indirect(ca_sb[:]))
+        nc.vector.tensor_copy(dealt(cb_s[:]), listed(cb_g[:]))
+        pair_w = reuse.tile([P, 2, C], U32, name="pair_w", align_bytes=64, offset=64)
+        cb_w = pair_w[:, 0, :]
+        ca_w = pair_w[:, 1, :]
+        nc.vector.tensor_copy(dealt(cb_w), xw[:].indirect(cb_sb[:]))
+        nc.vector.tensor_copy(dealt(ca_w), xw[:].indirect(ca_sb[:]))
 
         def product(out, lhs_w, lhs_s, t, rhs_w, rhs_s):
             cols = slice(t * P, (t + 1) * P)
@@ -133,14 +135,12 @@ def tile_picked_ccmpgatebgate_none_po_kernel(
                 i = Y_BANKS[h][t]
                 if i not in y_bank:
                     y_bank[i] = psum.tile([P, S], F32, name="y_ps", tag="bank%d" % i)
-                product(y_bank[i][:, cols], w1d_w, w1d_s, t, xq_w[:, cols], xq_s[:, cols])
-                if t < PACK - 1:
-                    nc.scalar.copy(y[t][:, cols], y_bank[i][:, cols])
-        nc.vector.tensor_copy(y[PACK - 1][:], y_bank[Y_BANKS[0][PACK - 1]][:])
+                product(y_bank[i][:, cols], w1d_w, w1d_s, t, xq_w[h][:], xq_s[:, cols])
+                nc.scalar.copy(y[t][:, cols], y_bank[i][:, cols])
 
-        ca_w = sb("ca_w", [P, C], U32, tag="xq_w")
-        nc.vector.tensor_copy(dealt(ca_w[:]), xw[:].indirect(ca_sb[:]))
-        deal(nc.vector, ca_s[:], ca_g[:])
+        ca_g = sb("ca_g", [P, C], U8, tag="xq_s")
+        nc.vector.tensor_copy(ca_g[:], xs[:].indirect(ca_sb[:]))
+        nc.vector.tensor_copy(dealt(ca_s[:]), listed(ca_g[:]))
 
         y_gate = {}
         for h, cols in enumerate(spans(Z_CHUNKS)):
@@ -167,10 +167,14 @@ def tile_picked_ccmpgatebgate_none_po_kernel(
             for i in sorted(set(B_BANKS[h])):
                 bank[i] = psum.tile([P, S], F32, name="b_ps", tag="bank%d" % i)
             b_ps = [bank[B_BANKS[h][t]][:, (t * w) % S : (t * w) % S + w] for t in range(PACK)]
-            for pair in PAIRS:
-                for t in pair:
+            if h < last:
+                for t in range(PACK):
                     product(b_ps[t], cb_w, cb_s, t, zq_w[:], zq_s[:])
-                for t in pair:
+                for t in range(PACK):
+                    product(a_ps[t][:, cols], ca_w, ca_s, t, zq_w[:], zq_s[:])
+            else:
+                for t in range(PACK):
+                    product(b_ps[t], cb_w, cb_s, t, zq_w[:], zq_s[:])
                     product(a_ps[t][:, cols], ca_w, ca_s, t, zq_w[:], zq_s[:])
             if h < last:
                 for t in range(PACK):
@@ -182,28 +186,27 @@ def tile_picked_ccmpgatebgate_none_po_kernel(
         o_s = sb("o_s", [P, S], U8)
         out_rows = out_0.rearrange("(p t) j -> p t j", t=PACK)
         out_words = out_1[0].rearrange("p n t -> p (n t)").bitcast(I32)
-        o = [sb("o%d" % h, [P, PACK, w], F32) for h, w in enumerate(OUT_CHUNKS)]
-        for pair in PAIRS:
-            for h, cols in enumerate(spans(OUT_CHUNKS)):
-                w = OUT_CHUNKS[h]
-                for t in pair:
-                    if h == 0:
-                        nc.scalar.copy(b[t][:, last_cols], last_b[t])
-                        if pair == PAIRS[0]:
-                            nc.vector.tensor_scalar(na[t][:, last_cols], a_ps[t][:, last_cols], -1.0 / 32, None, MULT)
-                        else:
-                            nc.scalar.activation(na[t][:, last_cols], a_ps[t][:, last_cols], COPY, scale=-1.0 / 32)
-                    gate = sb("b_gate%d_%d" % (t, h), [P, w], F32)
-                    nc.scalar.activation(gate[:], b[t][:].indirect(n3_sb[:, entries(cols)]), SIGMOID, scale=1.0 / 16)
-                    gated = sb("gated%d_%d" % (t, h), [P, w], F32)
-                    nc.vector.scalar_tensor_tensor(gated[:], na[t][:, cols], -2.0, gate[:], MULT, MULT)
-                    nc.vector.tensor_tensor(o[h][:, t, :], na[t][:].indirect(n2_sb[:, entries(cols)]), gated[:], ADD)
-                rows = slice(pair[0], pair[1] + 1)
-                nc.sync.dma_start(out_rows[:, rows, cols], o[h][:, rows, :])
+        outs = []
+        gated = [sb("gated%d" % t, [P, S], F32) for t in range(PACK)]
         for h, cols in enumerate(spans(OUT_CHUNKS)):
             w = OUT_CHUNKS[h]
+            o = sb("o%d" % h, [P, PACK, w], F32)
+            for t in range(PACK):
+                if h == 0:
+                    nc.scalar.copy(b[t][:, last_cols], last_b[t])
+                    nc.vector.tensor_scalar(na[t][:, last_cols], a_ps[t][:, last_cols], -1.0 / 32, None, MULT)
+                if h < len(GATE_CHUNKS):
+                    wide = spans(GATE_CHUNKS)[h]
+                    gate = sb("b_gate%d_%d" % (t, h), [P, GATE_CHUNKS[h]], F32)
+                    nc.scalar.activation(gate[:], b[t][:].indirect(n3_sb[:, entries(wide)]), SIGMOID, scale=1.0 / 16)
+                    nc.vector.scalar_tensor_tensor(gated[t][:, wide], na[t][:, wide], -2.0, gate[:], MULT, MULT)
+                nc.vector.tensor_tensor(o[:, t, :], na[t][:].indirect(n2_sb[:, entries(cols)]), gated[t][:, cols], ADD)
+            nc.sync.dma_start(out_rows[:, :, cols], o[:])
+            outs.append((h, cols, o))
+        for h, cols, o in outs:
+            w = OUT_CHUNKS[h]
             oi = sb("oi%d" % h, [P, PACK * w], BF16)
-            interleave(nc.scalar.copy if h < len(OUT_CHUNKS) - 1 else nc.vector.tensor_copy, oi[:], o[h][:])
+            interleave(nc.scalar.copy if h < len(OUT_CHUNKS) - 1 else nc.vector.tensor_copy, oi[:], o[:])
             o_w = sb("o_w%d" % h, [P, w], U32)
             nc.vector.quantize_mx(out=o_w[:].bitcast(FP8X4), scales=o_s[:, cols], in_=oi[:])
             nc.sync.dma_start(out_words[:, cols], o_w[:].bitcast(I32))

from contextlib import ExitStack

import concourse.mybir as mybir

K, T, S, H, C = 512, 2048, 512, 512, 512
FLOPS = 2 * K * H * S + 2 * 2 * K * C * S

F32 = mybir.dt.float32
BF16 = mybir.dt.bfloat16
I32 = mybir.dt.int32
U32 = mybir.dt.uint32
U16 = mybir.dt.uint16
U8 = mybir.dt.uint8
FP8X4 = mybir.dt.float8_e4m3fn_x4
MULT = mybir.AluOpType.mult
ADD = mybir.AluOpType.add
SIGMOID = mybir.ActivationFunctionType.Sigmoid
COPY = mybir.ActivationFunctionType.Copy

P = 128
PACK = 4
Y_CHUNKS = (256, 256)
Y_BANKS = ((4, 5, 6, 7), (0, 1, 2, 3))
Z_CHUNKS = (256, 256)
GATE_CHUNKS = (256, 256)
OUT_CHUNKS = (256, 128, 128)
B_BANKS = ((4, 4, 5, 5), (6, 7, 4, 5))


def spans(widths):
    starts = [sum(widths[:i]) for i in range(len(widths))]
    return [slice(s, s + w) for s, w in zip(starts, widths)]


def entries(cols):
    return slice(cols.start // 16, cols.stop // 16)


def interleave(engine_copy, dst, src):
    engine_copy(
        dst.rearrange("p (c i t) -> p c t i", i=4, t=PACK),
        src.rearrange("p t (c i) -> p c t i", i=4),
    )


def tile_picked_ccmpgatebgate_none_po_kernel(
    tc, x_words, x_scales, w1_words, w1_scales, gs, offs, n1, ca, cb, n2, n3, out_0, out_1, out_2
):
    nc = tc.nc
    with ExitStack() as ctx:
        lists = ctx.enter_context(tc.tile_pool(name="lists", bufs=1))
        keep = ctx.enter_context(tc.tile_pool(name="keep", bufs=1))
        reuse = ctx.enter_context(tc.tile_pool(name="reuse", bufs=1))
        psum = ctx.enter_context(tc.psum_pool(name="psum", bufs=1))

        def list_tile(name):
            return lists.tile([P, S // 16], U16, name=name)

        def sb(name, shape, dtype, tag=None):
            return keep.tile(shape, dtype, name=name, tag=tag or name, align_bytes=64)

        offs_sb, n1_sb, ca_sb, cb_sb, n2_sb, n3_sb = [list_tile(n) for n in ("offs_sb", "n1_sb", "ca_sb", "cb_sb", "n2_sb", "n3_sb")]
        xw = sb("xw", [P, T], U32)
        xs = sb("xs", [P, T], U8)
        w1w = sb("w1w", [P, H], U32)
        w1s = reuse.tile([P, H], U8, name="w1s", align_bytes=64, offset=4096)
        gs_sb = sb("gs_sb", [P, PACK], F32)
        warm = sb("warm", [P, 2], F32)

        nc.vector.memset(xs[:].bitcast(I32), 0)
        nc.gpsimd.memset(w1s[:].bitcast(I32), 0)
        nc.gpsimd.memset(warm[:, 0:1], 0.0)
        nc.scalar.activation(warm[:, 1:2], warm[:, 0:1], SIGMOID)

        nc.sync.dma_start(offs_sb[:], offs)
        nc.sync.dma_start(w1w[:].bitcast(I32), w1_words[0].rearrange("p n t -> p (n t)").bitcast(I32))
        for q in range(4):
            nc.sync.dma_start(xs[32 * q : 32 * q + 4, :].bitcast(I32), x_scales[0, 4 * q : 4 * q + 4, :].bitcast(I32))
        nc.sync.dma_start(cb_sb[:], cb)
        nc.sync.dma_start(xw[:].bitcast(I32), x_words[0].rearrange("p n t -> p (n t)").bitcast(I32))
        nc.sync.dma_start(ca_sb[:], ca)
        for q in range(4):
            nc.sync.dma_start(w1s[32 * q : 32 * q + 4, :].bitcast(I32), w1_scales[0, 4 * q : 4 * q + 4, :].bitcast(I32))
        nc.sync.dma_start(n1_sb[:], n1)
        nc.sync.dma_start(gs_sb[:], gs.rearrange("(p t) o -> p (t o)", t=PACK))
        nc.sync.dma_start(n3_sb[:], n3)
        nc.sync.dma_start(n2_sb[:], n2)

        def dealt(ap):
            return ap.rearrange("p (t m) -> p m t", t=PACK)

        def listed(ap):
            return ap.rearrange("p (m t) -> p m t", t=PACK)

        xq_s = sb("xq_s", [P, S], U8)
        w1d_w = sb("w1d_w", [P, H], U32)
        w1d_s = sb("w1d_s", [P, H], U8)
        cb_g = sb("cb_g", [P, C], U8)
        cb_s = sb("cb_s", [P, C], U8)
        ca_s = sb("ca_s", [P, C], U8)

        nc.vector.tensor_copy(xq_s[:], xs[:].indirect(offs_sb[:]))
        nc.vector.tensor_copy(dealt(w1d_w[:].bitcast(I32)), listed(w1w[:].bitcast(I32)))
        nc.vector.tensor_copy(dealt(w1d_s[:]), listed(w1s[:]))
        xq_w = [
            sb("xq_w0", [P, Y_CHUNKS[0]], U32),
            reuse.tile([P, Y_CHUNKS[1]], U32, name="xq_w1", align_bytes=64, offset=4544),
        ]
        for h, cols in enumerate(spans(Y_CHUNKS)):
            nc.vector.tensor_copy(xq_w[h][:], xw[:].indirect(offs_sb[:, entries(cols)]))
        nc.vector.tensor_copy(cb_g[:], xs[:].indirect(cb_sb[:]))
        nc.vector.tensor_copy(dealt(cb_s[:]), listed(cb_g[:]))
        pair_w = reuse.tile([P, 2, C], U32, name="pair_w", align_bytes=64, offset=64)
        cb_w = pair_w[:, 0, :]
        ca_w = pair_w[:, 1, :]
        nc.vector.tensor_copy(dealt(cb_w), xw[:].indirect(cb_sb[:]))
        nc.vector.tensor_copy(dealt(ca_w), xw[:].indirect(ca_sb[:]))

        def product(out, lhs_w, lhs_s, t, rhs_w, rhs_s):
            cols = slice(t * P, (t + 1) * P)
            nc.tensor.matmul_mx(
                out=out,
                lhsT=lhs_w[:, cols].bitcast(FP8X4),
                lhsT_scale=lhs_s[:, cols],
                rhs=rhs_w.bitcast(FP8X4),
                rhs_scale=rhs_s,
                start=True,
                stop=True,
            )

        y = [sb("y%d" % t, [P, S], F32) for t in range(PACK)]
        y_bank = {}
        for h, cols in enumerate(spans(Y_CHUNKS)):
            for t in range(PACK):
                i = Y_BANKS[h][t]
                if i not in y_bank:
                    y_bank[i] = psum.tile([P, S], F32, name="y_ps", tag="bank%d" % i)
                product(y_bank[i][:, cols], w1d_w, w1d_s, t, xq_w[h][:], xq_s[:, cols])
                nc.scalar.copy(y[t][:, cols], y_bank[i][:, cols])

        ca_g = sb("ca_g", [P, C], U8, tag="xq_s")
        nc.vector.tensor_copy(ca_g[:], xs[:].indirect(ca_sb[:]))
        nc.vector.tensor_copy(dealt(ca_s[:]), listed(ca_g[:]))

        y_gate = {}
        for h, cols in enumerate(spans(Z_CHUNKS)):
            for t in range(PACK):
                y_gate[h, t] = sb("y_gate%d_%d" % (h, t), [P, Z_CHUNKS[h]], F32)
                nc.scalar.activation(y_gate[h, t][:], y[t][:].indirect(n1_sb[:, entries(cols)]), SIGMOID)

        b = [sb("b%d" % t, [P, S], F32) for t in range(PACK)]
        na = [sb("na%d" % t, [P, S], F32) for t in range(PACK)]
        a_ps = [psum.tile([P, S], F32, name="a_ps", tag="bank%d" % t) for t in range(PACK)]
        last = len(Z_CHUNKS) - 1

        for h, cols in enumerate(spans(Z_CHUNKS)):
            w = Z_CHUNKS[h]
            z = sb("z%d" % h, [P, PACK, w], BF16, tag="z")
            for t in range(PACK):
                nc.vector.scalar_tensor_tensor(z[:, t, :], y[t][:, cols], gs_sb[:, t : t + 1], y_gate[h, t][:], MULT, MULT)
            zi = sb("zi%d" % h, [P, PACK * w], BF16)
            interleave(nc.vector.tensor_copy, zi[:], z[:])
            zq_w = sb("zq_w%d" % h, [P, w], U32)
            zq_s = sb("zq_s%d" % h, [P, w], U8)
            nc.vector.quantize_mx(out=zq_w[:].bitcast(FP8X4), scales=zq_s[:], in_=zi[:])
            bank = {}
            for i in sorted(set(B_BANKS[h])):
                bank[i] = psum.tile([P, S], F32, name="b_ps", tag="bank%d" % i)
            b_ps = [bank[B_BANKS[h][t]][:, (t * w) % S : (t * w) % S + w] for t in range(PACK)]
            if h < last:
                for t in range(PACK):
                    product(b_ps[t], cb_w, cb_s, t, zq_w[:], zq_s[:])
                for t in range(PACK):
                    product(a_ps[t][:, cols], ca_w, ca_s, t, zq_w[:], zq_s[:])
            else:
                for t in range(PACK):
                    product(b_ps[t], cb_w, cb_s, t, zq_w[:], zq_s[:])
                    product(a_ps[t][:, cols], ca_w, ca_s, t, zq_w[:], zq_s[:])
            if h < last:
                for t in range(PACK):
                    nc.scalar.copy(b[t][:, cols], b_ps[t])
                for t in range(PACK):
                    nc.scalar.activation(na[t][:, cols], a_ps[t][:, cols], COPY, scale=-1.0 / 32)
        last_cols, last_b = cols, b_ps

        o_s = sb("o_s", [P, S], U8)
        out_rows = out_0.rearrange("(p t) j -> p t j", t=PACK)
        out_words = out_1[0].rearrange("p n t -> p (n t)").bitcast(I32)
        outs = []
        gated = [sb("gated%d" % t, [P, S], F32) for t in range(PACK)]
        for h, cols in enumerate(spans(OUT_CHUNKS)):
            w = OUT_CHUNKS[h]
            o = sb("o%d" % h, [P, PACK, w], F32)
            for t in range(PACK):
                if h == 0:
                    nc.scalar.copy(b[t][:, last_cols], last_b[t])
                    nc.vector.tensor_scalar(na[t][:, last_cols], a_ps[t][:, last_cols], -1.0 / 32, None, MULT)
                if h < len(GATE_CHUNKS):
                    wide = spans(GATE_CHUNKS)[h]
                    gate = sb("b_gate%d_%d" % (t, h), [P, GATE_CHUNKS[h]], F32)
                    nc.scalar.activation(gate[:], b[t][:].indirect(n3_sb[:, entries(wide)]), SIGMOID, scale=1.0 / 16)
                    nc.vector.scalar_tensor_tensor(gated[t][:, wide], na[t][:, wide], -2.0, gate[:], MULT, MULT)
                nc.vector.tensor_tensor(o[:, t, :], na[t][:].indirect(n2_sb[:, entries(cols)]), gated[t][:, cols], ADD)
            nc.sync.dma_start(out_rows[:, :, cols], o[:])
            outs.append((h, cols, o))
        for h, cols, o in outs:
            w = OUT_CHUNKS[h]
            oi = sb("oi%d" % h, [P, PACK * w], BF16)
            interleave(nc.scalar.copy if h < len(OUT_CHUNKS) - 1 else nc.vector.tensor_copy, oi[:], o[:])
            o_w = sb("o_w%d" % h, [P, w], U32)
            nc.vector.quantize_mx(out=o_w[:].bitcast(FP8X4), scales=o_s[:, cols], in_=oi[:])
            nc.sync.dma_start(out_words[:, cols], o_w[:].bitcast(I32))
        for q in range(4):
            queue = nc.scalar if q % 2 else nc.sync
            queue.dma_start(out_2[0, 4 * q : 4 * q + 4, :].bitcast(I32), o_s[32 * q : 32 * q + 4, :].bitcast(I32))
